import numpy as np
import ml_dtypes


def mxq(x, axis, fmt="e4m3"):
    dtype, down = {"e4m3": (ml_dtypes.float8_e4m3fn, 7), "e5m2": (ml_dtypes.float8_e5m2, 14)}[fmt]
    v = np.moveaxis(np.asarray(x, np.float32).astype(ml_dtypes.bfloat16).astype(np.float64), axis, -1)
    blocks = v.reshape(v.shape[:-1] + (-1, 32))
    amax = np.abs(blocks).max(-1, keepdims=True)
    byte = np.maximum(np.where(amax > 0, np.frexp(amax)[1] - 1 + 127, 0) - down, 1)
    scale = np.exp2(byte - 127.0)
    codes = (blocks / scale).astype(np.float32).astype(dtype).astype(np.float64)
    return np.moveaxis((codes * scale).reshape(v.shape), -1, axis)


WIDE = False


def mx_kscale(k):
    if not WIDE:
        return np.ones(k)
    levels = np.array([10, -10, 5, -5, 0])
    if k % 512:
        return np.exp2(np.random.permutation(np.resize(levels, k // 32))).repeat(32)
    a = np.empty((k // 512, 16))
    for p in range(k // 512):
        a[p, :8] = np.random.permutation(np.resize(levels, 8))
        for g in range(8):
            far = levels[np.abs(levels - a[p, g]) >= 10]
            a[p, g + 8] = far[np.random.randint(len(far))]
    return np.exp2(a.ravel()).repeat(32)


def f64(x):
    return np.asarray(x).astype(np.float64)


def striped8(idx):
    return np.asarray(idx).reshape(8, -1, 16).transpose(0, 2, 1).reshape(128, -1).astype(np.uint16)


def unstriped8(offs):
    return offs.reshape(8, 16, -1).transpose(0, 2, 1).reshape(8, -1).astype(np.int64)


def pick8(x, idx, run):
    r = np.arange(len(x))
    return x[r[:, None], idx[r % (8 * run) // run]]


E2M1 = np.array([0.0, 0.5, 1.0, 1.5, 2.0, 3.0, 4.0, 6.0, -0.0, -0.5, -1.0, -1.5, -2.0, -3.0, -4.0, -6.0])


def pack_weight(w, fmt):
    k, n = w.shape
    w = f64(np.asarray(w, np.float32).astype(ml_dtypes.bfloat16)).reshape(k // 32, 32, n)
    amax = np.abs(w).max(1)
    if fmt == "e4m3":
        byte = np.frexp(amax)[1] - 1 + 127 - 7
    else:
        mant, ex = np.frexp(amax / 6.0)
        byte = np.where(mant > 0.5, ex, ex - 1) + 127
    byte = np.clip(np.where(amax > 0, byte, 1), 1, 254)
    scaled = (w * np.exp2(127.0 - byte)[:, None, :]).reshape(k, n).astype(np.float32)
    by_word = np.ascontiguousarray(scaled.reshape(k // 512, 128, 4, n).transpose(0, 1, 3, 2))
    if fmt == "e4m3":
        words = by_word.astype(ml_dtypes.float8_e4m3fn).view(np.uint8)
    else:
        c = by_word.astype(ml_dtypes.float4_e2m1fn).view(np.uint8) & 0xF
        words = (c[..., 0::2] | (c[..., 1::2] << 4)).reshape(k // 512, 128, 2 * n)
    return np.ascontiguousarray(words), np.ascontiguousarray(byte.astype(np.uint8).reshape(k // 512, 16, n))


def unpack_weight(words, scales, fmt):
    g, _, n = scales.shape
    words = np.ascontiguousarray(words).reshape(g, 128, n, -1)
    if fmt == "e4m3":
        vals = words.view(ml_dtypes.float8_e4m3fn).astype(np.float64)
    else:
        nib = np.empty((g, 128, n, 4), np.uint8)
        nib[..., 0::2] = words & 0xF
        nib[..., 1::2] = words >> 4
        vals = E2M1[nib]
    vals = vals * np.repeat(np.exp2(scales.astype(np.float64) - 127.0), 8, axis=1)[..., None]
    return vals.transpose(0, 1, 3, 2).reshape(g * 512, n)


D, T, U, I, Q = 512, 1024, 1024, 512, 128


def setup_inputs():
    n = np.random.standard_normal
    idx = np.stack([np.random.permutation(T)[:I] for _ in range(8)])
    idx2 = np.stack([np.random.permutation(U)[:I] for _ in range(8)])
    idx3 = np.stack([np.random.permutation(U)[:I] for _ in range(8)])
    fd = mx_kscale(D)
    keysp = pack_weight(n((D, T)) / fd[:, None], "e2m1")
    notesp = pack_weight(n((D, U)) / fd[:, None], "e4m3")
    return {
        "query": (n((D, Q)) * 1.0 / np.sqrt(D) * fd[:, None]).astype(np.float32),
        "keys_words": keysp[0],
        "keys_scales": keysp[1],
        "notes_words": notesp[0],
        "notes_scales": notesp[1],
        "offs": striped8(idx),
        "offs2": striped8(idx2),
        "offs3": striped8(idx3),
    }


def reference(query, keys_words, keys_scales, notes_words, notes_scales, offs, offs2, offs3):
    idx = unstriped8(offs)
    idx2 = unstriped8(offs2)
    idx3 = unstriped8(offs3)
    keysu = unpack_weight(keys_words, keys_scales, "e2m1")
    notesu = unpack_weight(notes_words, notes_scales, "e4m3")
    queryq = mxq(f64(query), 0, "e4m3")
    a = queryq.T @ keysu
    b = queryq.T @ notesu
    w = pick8(a, idx, 16) * 1.5
    w1 = np.pad(w, ((0, 0), (1, 0)))[:, :I]
    r = w - w1
    f1 = np.zeros((Q, U))
    f1[np.arange(Q)[:, None], idx2[np.arange(Q) % 128 // 16]] = r
    cc = b + f1
    y = pick8(cc, idx3, 16)
    return y

from contextlib import ExitStack

import concourse.mybir as mybir

D, T, U, I, Q = 512, 1024, 1024, 512, 128
FLOPS = 2 * D * Q * (T + U)

F32 = mybir.dt.float32
BF16 = mybir.dt.bfloat16
I32 = mybir.dt.int32
U32 = mybir.dt.uint32
U16 = mybir.dt.uint16
U8 = mybir.dt.uint8
FP8X4 = mybir.dt.float8_e4m3fn_x4
FP4X4 = mybir.dt.float4_e2m1fn_x4
ADD = mybir.AluOpType.add
MULT = mybir.AluOpType.mult
COPY = mybir.ActivationFunctionType.Copy

P = 128
PACK = 4
HALF = I // 2
HALF_COLS = HALF // 16
PAD = 8
A_PIECE = 256
BANK = 512


def load_scale_rows(nc, plane, scales):
    for quad in range(4):
        nc.sync.dma_start(
            out=plane[32 * quad : 32 * quad + 4, :].bitcast(I32),
            in_=scales[0, 4 * quad : 4 * quad + 4, :].bitcast(I32),
        )


def tile_attend_stepsbetween_two_kernel(
    tc, query, keys_words, keys_scales, notes_words, notes_scales, offs, offs2, offs3, out
):
    nc = tc.nc
    with ExitStack() as ctx:
        lists = ctx.enter_context(tc.tile_pool(name="lists", bufs=1))
        keep = ctx.enter_context(tc.tile_pool(name="keep", bufs=1))
        psum = ctx.enter_context(tc.psum_pool(name="psum", bufs=1))

        key_plane = keep.tile([P, T], U8, align_bytes=64, name="key_plane")
        nc.vector.memset(key_plane[:].bitcast(U32), 0)

        raw = keep.tile([P, PACK, Q], F32, align_bytes=64, name="raw", tag="first_raw")
        nc.sync.dma_start(out=raw[:], in_=query.rearrange("(p j) q -> p j q", j=PACK))
        key_codes = keep.tile([P, 2 * T], U8, align_bytes=64, name="key_codes")
        nc.scalar.dma_start(out=key_codes[:].bitcast(I32), in_=keys_words[0].bitcast(I32))
        load_scale_rows(nc, key_plane, keys_scales)
        token_list = lists.tile([P, I // 16], U16, name="token_list")
        nc.sync.dma_start(token_list[:], offs)
        put_list = lists.tile([P, I // 16], U16, name="put_list")
        nc.sync.dma_start(put_list[:], offs2)
        take_list = lists.tile([P, I // 16], U16, name="take_list")
        nc.sync.dma_start(take_list[:], offs3)

        f1 = keep.tile([P, U], F32, name="f1")
        nc.vector.memset(f1[:], 0.0)
        neg = keep.tile([P, PAD + I], F32, name="neg")
        nc.scalar.activation(neg[:, PAD - 1 : PAD], f1[:, 0:1], COPY)

        grouped = keep.tile([P, Q, PACK], BF16, align_bytes=64, name="grouped", tag="first_grouped")
        nc.vector.tensor_copy(out=grouped[:], in_=raw[:].rearrange("p j q -> p q j"))
        q_codes = keep.tile([P, Q], U32, align_bytes=64, name="q_codes")
        q_plane = keep.tile([P, Q], U8, align_bytes=64, name="q_plane")
        nc.vector.quantize_mx(
            out=q_codes[:].bitcast(FP8X4),
            scales=q_plane[:],
            in_=grouped[:].rearrange("p q j -> p (q j)"),
        )

        a = keep.tile([P, T], F32, name="a")
        for piece in range(T // A_PIECE):
            c0, c1 = piece * A_PIECE, (piece + 1) * A_PIECE
            a_bank = psum.tile([P, A_PIECE], F32, name="a_bank%d" % piece)
            nc.tensor.matmul_mx(
                out=a_bank[:],
                lhsT=q_codes[:].bitcast(FP8X4),
                lhsT_scale=q_plane[:],
                rhs=key_codes[:, 2 * c0 : 2 * c1].bitcast(FP4X4),
                rhs_scale=key_plane[:, c0:c1],
                start=True,
                stop=True,
            )
            if piece % 2 == 0:
                nc.scalar.copy(a[:, c0:c1], a_bank[:])
            else:
                nc.vector.tensor_copy(a[:, c0:c1], a_bank[:])

        note_codes = keep.tile([P, U], U32, align_bytes=64, name="note_codes", tag="first_raw")
        nc.sync.dma_start(
            out=note_codes[:].bitcast(I32),
            in_=notes_words[0].rearrange("p n t -> p (n t)").bitcast(I32),
        )
        note_plane = keep.tile([P, U], U8, align_bytes=64, name="note_plane", tag="first_grouped")
        nc.vector.memset(note_plane[:].bitcast(U32), 0)
        load_scale_rows(nc, note_plane, notes_scales)

        w_lo = keep.tile([P, HALF], F32, name="w_lo")
        w_hi = keep.tile([P, HALF], F32, name="w_hi")
        nc.vector.tensor_scalar(
            w_lo[:], a[:].indirect(token_list[:, 0:HALF_COLS]), 1.5, 0.0, MULT, ADD
        )
        nc.scalar.activation(
            neg[:, PAD : PAD + HALF], a[:].indirect(token_list[:, 0:HALF_COLS]), COPY, scale=-1.5
        )
        nc.scalar.activation(
            w_hi[:], a[:].indirect(token_list[:, HALF_COLS : 2 * HALF_COLS]), COPY, scale=1.5
        )
        nc.scalar.activation(
            neg[:, PAD + HALF : PAD + I - 1], w_hi[:, 0 : HALF - 1], COPY, scale=-1.0
        )

        nc.vector.tensor_tensor(
            f1[:].indirect(put_list[:, 0:HALF_COLS]),
            w_lo[:],
            neg[:, PAD - 1 : PAD - 1 + HALF],
            ADD,
        )
        nc.vector.tensor_tensor(
            f1[:].indirect(put_list[:, HALF_COLS : 2 * HALF_COLS]),
            w_hi[:],
            neg[:, PAD - 1 + HALF : PAD - 1 + I],
            ADD,
        )

        cc = keep.tile([P, U], F32, name="cc")
        for piece in range(U // BANK):
            c0, c1 = piece * BANK, (piece + 1) * BANK
            b_bank = psum.tile([P, BANK], F32, name="b_bank%d" % piece)
            nc.tensor.matmul_mx(
                out=b_bank[:],
                lhsT=q_codes[:].bitcast(FP8X4),
                lhsT_scale=q_plane[:],
                rhs=note_codes[:, c0:c1].bitcast(FP8X4),
                rhs_scale=note_plane[:, c0:c1],
                start=True,
                stop=True,
            )
            nc.vector.tensor_tensor(cc[:, c0:c1], f1[:, c0:c1], b_bank[:], ADD)

        y_lo = keep.tile([P, HALF], F32, name="y_lo")
        y_hi = keep.tile([P, HALF], F32, name="y_hi")
        nc.vector.tensor_copy(y_lo[:], cc[:].indirect(take_list[:, 0:HALF_COLS]))
        nc.scalar.activation(
            y_hi[:], cc[:].indirect(take_list[:, HALF_COLS : 2 * HALF_COLS]), COPY
        )
        nc.sync.dma_start(out=out[:, 0:HALF], in_=y_lo[:])
        nc.scalar.dma_start(out=out[:, HALF:I], in_=y_hi[:])
